import numpy as np
import ml_dtypes


def mxq(x, axis, fmt="e4m3"):
    dtype, down = {"e4m3": (ml_dtypes.float8_e4m3fn, 7), "e5m2": (ml_dtypes.float8_e5m2, 14)}[fmt]
    v = np.moveaxis(np.asarray(x, np.float32).astype(ml_dtypes.bfloat16).astype(np.float64), axis, -1)
    blocks = v.reshape(v.shape[:-1] + (-1, 32))
    amax = np.abs(blocks).max(-1, keepdims=True)
    byte = np.maximum(np.where(amax > 0, np.frexp(amax)[1] - 1 + 127, 0) - down, 1)
    scale = np.exp2(byte - 127.0)
    codes = (blocks / scale).astype(np.float32).astype(dtype).astype(np.float64)
    return np.moveaxis((codes * scale).reshape(v.shape), -1, axis)


WIDE = False


def mx_kscale(k):
    if not WIDE:
        return np.ones(k)
    levels = np.array([10, -10, 5, -5, 0])
    if k % 512:
        return np.exp2(np.random.permutation(np.resize(levels, k // 32))).repeat(32)
    a = np.empty((k // 512, 16))
    for p in range(k // 512):
        a[p, :8] = np.random.permutation(np.resize(levels, 8))
        for g in range(8):
            far = levels[np.abs(levels - a[p, g]) >= 10]
            a[p, g + 8] = far[np.random.randint(len(far))]
    return np.exp2(a.ravel()).repeat(32)


def f64(x):
    return np.asarray(x).astype(np.float64)


def striped(idx):
    return np.tile(idx.reshape(-1, 16).T, (8, 1)).astype(np.uint16)


def unstriped(offs):
    return offs[:16].T.reshape(-1).astype(np.int64)


def striped8(idx):
    return np.concatenate([x.reshape(-1, 16).T for x in idx]).astype(np.uint16)


def runs(offs, k):
    lists = np.stack([offs[16 * r : 16 * r + 16].T.reshape(-1) for r in range(8)]).astype(np.int64)
    return lists[np.arange(k) % 512 // 64]


def pack_weight(w):
    k, n = w.shape
    w = f64(np.asarray(w, np.float32).astype(ml_dtypes.bfloat16)).reshape(k // 32, 32, n)
    amax = np.abs(w).max(1)
    byte = np.clip(np.where(amax > 0, np.frexp(amax)[1] - 1 + 127 - 7, 1), 1, 254)
    scaled = (w * np.exp2(127.0 - byte)[:, None, :]).reshape(k, n).astype(np.float32)
    words = np.ascontiguousarray(scaled.reshape(k // 512, 128, 4, n).transpose(0, 1, 3, 2)).astype(ml_dtypes.float8_e4m3fn).view(np.uint8)
    return words, np.ascontiguousarray(byte.astype(np.uint8).reshape(k // 512, 16, n))


def unpack_weight(words, scales):
    g, p, n, _ = words.shape
    vals = np.ascontiguousarray(words).view(ml_dtypes.float8_e4m3fn).astype(np.float64) * np.repeat(np.exp2(scales.astype(np.float64) - 127.0), 8, axis=1)[..., None]
    return vals.transpose(0, 1, 3, 2).reshape(g * 512, n)


def sigmoid(v):
    return 1.0 / (1.0 + np.exp(-np.maximum(v, -700.0)))

def planes(y):
    n, m = y.shape
    v = y.astype(np.float32).astype(ml_dtypes.bfloat16).astype(np.float64).reshape(n // 32, 32, m)
    top = np.abs(v).max(1)
    byte = np.clip(np.where(top > 0, np.frexp(top)[1] - 1 + 127 - 7, 1), 1, 254)
    codes = (v * np.exp2(127.0 - byte)[:, None, :]).reshape(n, m).astype(np.float32).astype(ml_dtypes.float8_e4m3fn).view(np.uint8)
    words = codes.reshape(n // 512, 128, 4, m).transpose(0, 1, 3, 2)
    return np.ascontiguousarray(words), np.ascontiguousarray(byte.astype(np.uint8).reshape(n // 512, 16, m))


K, T, S, N, G, H, W = 512, 1024, 256, 512, 2048, 512, 1024


def setup_inputs():
    n = np.random.standard_normal
    s = mx_kscale(K)[:, None]
    u = mx_kscale(K)
    packed_xT = pack_weight(n((K, T)) * s)
    packed_dT = pack_weight(n((K, G)) / s)
    packed_w1 = pack_weight(n((H, N)) / np.sqrt(2 * H) / u[:, None])
    packed_w2 = pack_weight(n((H, N)) / np.sqrt(2 * H) / u[:, None])
    return {
        "x_words": packed_xT[0],
        "x_scales": packed_xT[1],
        "d_words": packed_dT[0],
        "d_scales": packed_dT[1],
        "gn": (np.random.uniform(0.5, 1.5, (H, 1)) * u[:, None]).astype(np.float32),
        "gm": (np.random.uniform(0.5, 1.5, (H, 1)) * u[:, None]).astype(np.float32),
        "w1_words": packed_w1[0],
        "w1_scales": packed_w1[1],
        "w2_words": packed_w2[0],
        "w2_scales": packed_w2[1],
        "offs": striped(np.random.permutation(T)[:S]),
        "k1": striped8(np.random.randint(0, G, (8, H))),
        "two": striped(np.random.permutation(T)[:S]),
        "n1": striped(np.random.randint(0, S, W)),
        "n2": striped8(np.stack([np.random.permutation(S) for _ in range(8)])),
        "n3": striped8(np.stack([np.random.permutation(S) for _ in range(8)])),
        "n4": striped(np.random.permutation(S)),
        "n5": striped(np.random.permutation(S)),
    }


def reference(x_words, x_scales, d_words, d_scales, gn, gm, w1_words, w1_scales, w2_words, w2_scales, offs, k1, two, n1, n2, n3, n4, n5):
    d_k1 = unpack_weight(d_words, d_scales)[np.arange(K)[:, None], runs(k1, K)]
    xq = unpack_weight(x_words, x_scales)[:, unstriped(offs)]
    a = 0.0625 * (d_k1.T @ xq)
    mb = a[:, unstriped(n1)]
    mx = mb.reshape(H, S, 4).max(axis=2)
    mn = mb.reshape(H, S, 4).min(axis=2)
    z = f64(gn) * (np.maximum(np.minimum(1.5 * a, mx), mn))
    x_two = unpack_weight(x_words, x_scales)[:, unstriped(two)]
    b = 0.0625 * (d_k1.T @ x_two)
    z2 = f64(gm) * (np.maximum(b * (sigmoid(b[np.arange(H)[:, None], runs(n2, H)])), b[np.arange(H)[:, None], runs(n3, H)]))
    h = unpack_weight(w1_words, w1_scales).T @ mxq(z, 0, "e4m3") + unpack_weight(w2_words, w2_scales).T @ mxq(z2, 0, "e4m3")
    out_0 = (h - h[:, unstriped(n4)]) / (np.abs(h[:, unstriped(n5)] - h) + 0.5)
    return (out_0,) + planes(out_0)

@@ -1,0 +1,283 @@
+from contextlib import ExitStack
+
+import concourse.mybir as mybir
+
+F32 = mybir.dt.float32
+BF16 = mybir.dt.bfloat16
+I32 = mybir.dt.int32
+U32 = mybir.dt.uint32
+U16 = mybir.dt.uint16
+U8 = mybir.dt.uint8
+FP8X4 = mybir.dt.float8_e4m3fn_x4
+ALU = mybir.AluOpType
+ACT = mybir.ActivationFunctionType
+
+P = 128
+PACK = 4
+T, G, S, H, MEMBERS = 1024, 2048, 256, 512, 4
+HALF = S // 2
+QUART = S // 4
+A_WIN = 528
+B_WIN = 512
+FLOPS = 2 * 512 * 512 * 256 * 4
+
+
+def words_of(dram):
+    return dram[0].rearrange("p n t -> p (n t)").bitcast(I32)
+
+
+def deal(nc, dst, src):
+    nc.vector.tensor_copy(
+        out=dst.rearrange("p (t m) -> p m t", t=PACK), in_=src.rearrange("p (m t) -> p m t", t=PACK)
+    )
+
+
+def walk_src(ap):
+    return ap.rearrange("p (t c i) -> p c t i", t=PACK, i=4)
+
+
+def walk_dst(ap):
+    return ap.rearrange("p (c i t) -> p c t i", t=PACK, i=4)
+
+
+def tile_picked_kjgclipgmaxfrac_none_po_kernel(
+    tc, x_words, x_scales, d_words, d_scales, gn, gm, w1_words, w1_scales, w2_words, w2_scales,
+    offs, k1, two, n1, n2, n3, n4, n5, out_0, out_1, out_2,
+):
+    nc = tc.nc
+    with ExitStack() as ctx:
+        lists = ctx.enter_context(tc.tile_pool(name="lists", bufs=1))
+        sb = ctx.enter_context(tc.tile_pool(name="sb", bufs=1))
+        ps = ctx.enter_context(tc.psum_pool(name="ps", bufs=1))
+
+        def list_tile(name, dram):
+            tl = lists.tile(list(dram.shape), U16, name=name)
+            nc.sync.dma_start(tl[:], dram)
+            return tl
+
+        def sbt(name, shape, dtype, tag=None):
+            return sb.tile(shape, dtype, name=name, tag=tag or name, align_bytes=64)
+
+        d_win = sbt("d_win", [P, G], U32)
+        x_win = sbt("x_win", [P, T], U32)
+        ds_win = sbt("ds_win", [P, G], U8)
+        xs_win = sbt("xs_win", [P, T], U8)
+        ds_plane = sbt("ds_plane", [P, H], U8)
+        a_win = [sbt(f"a_win{t}", [P, A_WIN], F32) for t in range(PACK)]
+        b_win = [sbt(f"b_win{t}", [P, B_WIN], F32) for t in range(PACK)]
+        h_all = sbt("h_all", [P, (PACK + 1) * S], F32)
+        half_col = sbt("half_col", [P, 1], F32)
+
+        nc.vector.memset(ds_plane[:].bitcast(I32), 0)
+
+        nc.scalar.dma_start(d_win[:].bitcast(I32), words_of(d_words))
+        k1_l = list_tile("k1_l", k1)
+        nc.scalar.dma_start(x_win[:].bitcast(I32), words_of(x_words))
+        nc.sync.dma_start(ds_win[:].bitcast(I32), d_scales[0].bitcast(I32).unsqueeze(1).to_broadcast([16, 8, G // 4]))
+        offs_l = list_tile("offs_l", offs)
+        for q in range(4):
+            rows = x_scales[0, 4 * q : 4 * q + 4, :].bitcast(I32)
+            eng = nc.sync if q == 0 else nc.gpsimd
+            eng.dma_start(xs_win[32 * q : 32 * q + 32, :].bitcast(I32), rows.unsqueeze(0).to_broadcast([8, 4, T // 4]))
+        two_l = list_tile("two_l", two)
+        n1_l = list_tile("n1_l", n1)
+        n2_l = list_tile("n2_l", n2)
+        n3_l = list_tile("n3_l", n3)
+        n4_l = list_tile("n4_l", n4)
+        n5_l = list_tile("n5_l", n5)
+        gn_t = sbt("gn_t", [P, PACK], F32)
+        gm_t = sbt("gm_t", [P, PACK], F32)
+        nc.gpsimd.dma_start(gn_t[:], gn.rearrange("(p t) o -> p (t o)", t=PACK))
+        nc.gpsimd.dma_start(gm_t[:], gm.rearrange("(p t) o -> p (t o)", t=PACK))
+
+        for t in range(PACK):
+            nc.vector.memset(a_win[t][:, S:], 0.0)
+        for t in range(PACK):
+            nc.vector.memset(b_win[t][:, S:], 0.0)
+        nc.vector.memset(h_all[:, PACK * S :], 0.0)
+        nc.vector.memset(half_col[:], 0.5)
+
+        ds_got = sbt("ds_got", [P, H], U8, tag="ds_got_then_w")
+        nc.vector.tensor_copy(out=ds_got[:], in_=ds_win[:].indirect(k1_l[:]))
+        ds_dealt = sbt("ds_dealt", [P, H], U8, tag="ds_dealt_then_ws")
+        deal(nc, ds_dealt[:], ds_got[:])
+        for b in range(4):
+            nc.scalar.dma_start(ds_plane[b:P:32, :].bitcast(I32), ds_dealt[8 * b : P : 32, :].bitcast(I32))
+        w_raw = sbt("w_raw", [P, 2 * H], U32, tag="ds_got_then_w")
+        nc.sync.dma_start(w_raw[:, :H].bitcast(I32), words_of(w1_words))
+        nc.sync.dma_start(w_raw[:, H:].bitcast(I32), words_of(w2_words))
+        ws_raw = sbt("ws_raw", [P, H], U8, tag="ds_dealt_then_ws")
+        nc.gpsimd.memset(ws_raw[:].bitcast(I32), 0)
+        for k, scales in enumerate((w1_scales, w2_scales)):
+            for q in range(4):
+                r0 = 32 * q + 4 * k
+                nc.sync.dma_start(ws_raw[r0 : r0 + 4, :].bitcast(I32), scales[0, 4 * q : 4 * q + 4, :].bitcast(I32))
+
+        xb_s = sbt("xb_s", [P, S], U8)
+        xa_w = sbt("xa_w", [P, S], U32)
+        xb_w = sbt("xb_w", [P, S], U32)
+        d_got = sbt("d_got", [P, H], U32, tag="d_got_then_xa_s")
+        d_dealt = sbt("d_dealt", [P, H], U32)
+        nc.vector.tensor_copy(out=d_got[:], in_=d_win[:].indirect(k1_l[:]))
+        deal(nc, d_dealt[:].bitcast(I32), d_got[:].bitcast(I32))
+        xa_s = sbt("xa_s", [P, S], U8, tag="d_got_then_xa_s")
+        nc.vector.tensor_copy(out=xa_s[:], in_=xs_win[:].indirect(offs_l[:]))
+        nc.vector.tensor_copy(out=xa_w[:], in_=x_win[:].indirect(offs_l[:]))
+        gn16 = sbt("gn16", [P, PACK], F32)
+        nc.vector.tensor_scalar(out=gn16[:], in0=gn_t[:], scalar1=0.0625, scalar2=None, op0=ALU.mult)
+
+        def score(out, t, xw, xs):
+            cols = slice(t * P, (t + 1) * P)
+            nc.tensor.matmul_mx(
+                out=out, lhsT=d_dealt[:, cols].bitcast(FP8X4), lhsT_scale=ds_plane[:, cols],
+                rhs=xw[:].bitcast(FP8X4), rhs_scale=xs[:], start=True, stop=True,
+            )
+
+        a_ps0 = ps.tile([P, S], F32, name="a_ps0")
+        a_ps1 = ps.tile([P, S], F32, name="a_ps1")
+        a_ps23 = ps.tile([P, 2, S], F32, name="a_ps23")
+        a_ps = [a_ps0[:], a_ps1[:], a_ps23[:, 0, :], a_ps23[:, 1, :]]
+        for t in range(PACK):
+            score(a_ps[t], t, xa_w, xa_s)
+        for t in range(PACK):
+            nc.scalar.activation(out=a_win[t][:, :S], in_=a_ps[t], func=ACT.Copy, scale=gn16[:, t : t + 1])
+
+        nc.vector.tensor_copy(out=xb_w[:], in_=x_win[:].indirect(two_l[:]))
+        nc.vector.tensor_copy(out=xb_s[:], in_=xs_win[:].indirect(two_l[:]))
+        b_ps = [ps.tile([P, 2, S], F32, name=f"b_ps{u}") for u in range(2)]
+        for t in range(PACK):
+            score(b_ps[t // 2][:, t % 2, :], t, xb_w, xb_s)
+
+        w_dealt = sbt("w_dealt", [P, 2 * H], U32)
+        ws_plane = sbt("ws_plane", [P, H], U8)
+        for k in range(2):
+            deal(nc, w_dealt[:, k * H : (k + 1) * H].bitcast(I32), w_raw[:, k * H : (k + 1) * H].bitcast(I32))
+        lower = sbt("lower", [P, PACK * S], F32)
+        capped = sbt("capped", [P, PACK * S], F32)
+        for t in range(PACK):
+            mb = sbt(f"mb{t}", [P, MEMBERS * S], F32)
+            for u in range(2):
+                nc.scalar.activation(
+                    out=mb[:, u * 512 : (u + 1) * 512], in_=a_win[t][:].indirect(n1_l[:, u * 32 : (u + 1) * 32]), func=ACT.Copy
+                )
+            pairs = mb[:].rearrange("p (j u e) -> p j u e", u=2, e=2)
+            hi = sbt(f"hi{t}", [P, S, 2], F32)
+            lo = sbt(f"lo{t}", [P, S, 2], F32)
+            upper = sbt(f"upper{t}", [P, S], F32)
+            cols = slice(t * S, (t + 1) * S)
+            nc.vector.tensor_tensor(out=hi[:], in0=pairs[:, :, 0, :], in1=pairs[:, :, 1, :], op=ALU.max)
+            nc.vector.tensor_tensor(out=lo[:], in0=pairs[:, :, 0, :], in1=pairs[:, :, 1, :], op=ALU.min)
+            nc.vector.tensor_tensor(out=upper[:], in0=hi[:, :, 0], in1=hi[:, :, 1], op=ALU.max)
+            nc.vector.tensor_tensor(out=lower[:, cols], in0=lo[:, :, 0], in1=lo[:, :, 1], op=ALU.min)
+            nc.vector.scalar_tensor_tensor(
+                out=capped[:, cols], in0=a_win[t][:, :S], scalar=1.5, in1=upper[:], op0=ALU.mult, op1=ALU.min
+            )
+        deal(nc, ws_plane[:], ws_raw[:])
+        z_bf = sbt("z_bf", [P, S * PACK], BF16)
+        nc.vector.tensor_tensor(out=walk_dst(z_bf[:]), in0=walk_src(capped[:]), in1=walk_src(lower[:]), op=ALU.max)
+        z_codes = sbt("z_codes", [P, S], U32)
+        z_plane = sbt("z_plane", [P, S], U8)
+        nc.vector.quantize_mx(out=z_codes[:].bitcast(FP8X4), scales=z_plane[:], in_=z_bf[:])
+
+        for t in range(PACK):
+            nc.scalar.activation(out=b_win[t][:, :S], in_=b_ps[t // 2][:, t % 2, :], func=ACT.Copy, scale=0.0625)
+
+        h_view = h_all[:, : PACK * S].rearrange("p (t j) -> p t j", t=PACK)
+        h_ps = [
+            [ps.tile([P, PACK, HALF], F32, name="h_ps0")],
+            [ps.tile([P, 2, HALF], F32, name="h_ps1a"), ps.tile([P, 2, HALF], F32, name="h_ps1b")],
+        ]
+        gm_b = gm_t[:].unsqueeze(1).unsqueeze(3).to_broadcast([P, HALF // 4, PACK, 4])
+        for u in range(2):
+            js = slice(u * HALF, (u + 1) * HALF)
+            ls = slice(u * HALF // 16, (u + 1) * HALF // 16)
+            gate = sbt(f"gate{u}", [P, PACK, HALF], F32)
+            other = sbt(f"other{u}", [P, PACK * HALF], F32)
+            for t in range(PACK):
+                nc.scalar.activation(out=gate[:, t, :], in_=b_win[t][:].indirect(n2_l[:, ls]), func=ACT.Sigmoid)
+            for t in range(PACK):
+                nc.scalar.activation(
+                    out=other[:, t * HALF : (t + 1) * HALF], in_=b_win[t][:].indirect(n3_l[:, ls]), func=ACT.Copy
+                )
+            gated = sbt(f"gated{u}", [P, PACK, HALF], F32)
+            for v in range(2):
+                nc.vector.scalar_tensor_tensor(
+                    out=gated[:, 2 * v : 2 * v + 2, :], in0=b_ps[v][:, :, js], scalar=0.0625,
+                    in1=gate[:, 2 * v : 2 * v + 2, :], op0=ALU.mult, op1=ALU.mult,
+                )
+            larger = sbt(f"larger{u}", [P, PACK * HALF], F32)
+            gated_flat = gated[:].rearrange("p t j -> p (t j)")
+            for c in (slice(0, 3 * HALF), slice(3 * HALF, 4 * HALF)):
+                nc.vector.tensor_tensor(out=larger[:, c], in0=gated_flat[:, c], in1=other[:, c], op=ALU.max)
+            z2_bf = sbt(f"z2_bf{u}", [P, HALF * PACK], BF16)
+            nc.vector.tensor_tensor(out=walk_dst(z2_bf[:]), in0=walk_src(larger[:]), in1=gm_b, op=ALU.mult)
+            z2_codes = sbt(f"z2_codes{u}", [P, HALF], U32)
+            z2_plane = sbt(f"z2_plane{u}", [P, HALF], U8)
+            nc.vector.quantize_mx(out=z2_codes[:].bitcast(FP8X4), scales=z2_plane[:], in_=z2_bf[:])
+            per_bank = PACK // len(h_ps[u])
+            for k, (codes, plane) in enumerate(((z_codes[:, js], z_plane[:, js]), (z2_codes[:], z2_plane[:]))):
+                for t in range(PACK):
+                    nc.tensor.matmul_mx(
+                        out=h_ps[u][t // per_bank][:, t % per_bank, :],
+                        lhsT=w_dealt[:, k * H + t * P : k * H + (t + 1) * P].bitcast(FP8X4),
+                        lhsT_scale=ws_plane[4 * k : P, t * P : (t + 1) * P],
+                        rhs=codes.bitcast(FP8X4), rhs_scale=plane,
+                        start=(k == 0 and t % per_bank == 0), stop=(k == 1 and t % per_bank == per_bank - 1),
+                    )
+            if u == 0:
+                nc.scalar.copy(out=h_view[:, :, js], in_=h_ps[0][0][:])
+            else:
+                nc.scalar.copy(out=h_view[:, 0:2, js], in_=h_ps[1][0][:])
+                nc.vector.tensor_copy(out=h_view[:, 2:4, js], in_=h_ps[1][1][:])
+
+        far, near, numer, y = [sbt(n, [P, PACK, S], F32) for n in ("far", "near", "numer", "y")]
+        diff, dist, logs = [sbt(n, [P, 4, PACK, QUART], F32) for n in ("diff", "dist", "logs")]
+        pieces = [slice(0, 2), slice(2, 3), slice(3, 4)]
+
+        def cols_of(qs, width):
+            return slice(qs.start * width, qs.stop * width)
+
+        def by_quarter(ap):
+            return ap.rearrange("p t (q c) -> p q t c", c=QUART)
+
+        def flat(ap):
+            return ap.rearrange("p q t c -> p (q t c)")
+
+        for qs in pieces:
+            js = cols_of(qs, QUART)
+            for t in range(PACK):
+                window = h_all[:, t * S : (t + 2) * S]
+                nc.scalar.activation(out=far[:, t, js], in_=window.indirect(n5_l[:, cols_of(qs, QUART // 16)]), func=ACT.Copy)
+            nc.vector.tensor_tensor(
+                out=diff[:, qs], in0=by_quarter(far[:, :, js]), in1=by_quarter(h_view[:, :, js]), op=ALU.subtract
+            )
+            nc.vector.scalar_tensor_tensor(
+                out=flat(dist[:, qs]), in0=flat(diff[:, qs]), scalar=-1.0, in1=flat(diff[:, qs]), op0=ALU.mult, op1=ALU.max
+            )
+        for qs in pieces:
+            nc.scalar.activation(out=flat(logs[:, qs]), in_=flat(dist[:, qs]), func=ACT.Ln, bias=half_col[:])
+        for u in range(2):
+            js = slice(u * HALF, (u + 1) * HALF)
+            ls = slice(u * HALF // 16, (u + 1) * HALF // 16)
+            for t in range(PACK):
+                nc.vector.tensor_copy(out=near[:, t, js], in_=h_all[:, t * S : (t + 2) * S].indirect(n4_l[:, ls]))
+            nc.vector.tensor_tensor(out=numer[:, :, js], in0=h_view[:, :, js], in1=near[:, :, js], op=ALU.subtract)
+        y_codes = sbt("y_codes", [P, S], U32)
+        y_plane = sbt("y_plane", [P, S], U8)
+        y_bf = sbt("y_bf", [P, S * PACK], BF16)
+        out_view = out_0.rearrange("(p t) j -> p t j", t=PACK)
+        recip = dist[:].rearrange("p t q c -> p t (q c)")
+        for qs in pieces:
+            js = cols_of(qs, QUART)
+            nc.scalar.activation(out=by_quarter(recip[:, :, js]), in_=logs[:, qs], func=ACT.Exp, scale=-1.0)
+            nc.vector.tensor_tensor(out=y[:, :, js], in0=numer[:, :, js], in1=recip[:, :, js], op=ALU.mult)
+            bf = y_bf[:, cols_of(qs, QUART * PACK)]
+            nc.vector.tensor_copy(out=walk_dst(bf), in_=y[:, :, js].rearrange("p t (c i) -> p c t i", i=4))
+            nc.vector.quantize_mx(out=y_codes[:, js].bitcast(FP8X4), scales=y_plane[:, js], in_=bf)
+            if qs.stop % 2 == 0:
+                hs = slice(js.stop - HALF, js.stop)
+                nc.sync.dma_start(out_view[:, :, hs], y[:, :, hs])
+                nc.sync.dma_start(words_of(out_1)[:, hs], y_codes[:, hs].bitcast(I32))
+        for q in range(4):
+            eng = nc.scalar if q % 2 else nc.sync
+            eng.dma_start(out_2[0, 4 * q : 4 * q + 4, :].bitcast(I32), y_plane[32 * q : 32 * q + 4, :].bitcast(I32))

@@ -68,6 +68,7 @@ def tile_picked_kjgclipgmaxfrac_none_po_kernel(
         h_all = sbt("h_all", [P, (PACK + 1) * S], F32)
         half_col = sbt("half_col", [P, 1], F32)
 
+        nc.vector.memset(half_col[:], 0.5)
         nc.vector.memset(ds_plane[:].bitcast(I32), 0)
 
         nc.scalar.dma_start(d_win[:].bitcast(I32), words_of(d_words))
@@ -95,8 +96,9 @@ def tile_picked_kjgclipgmaxfrac_none_po_kernel(
         for t in range(PACK):
             nc.vector.memset(b_win[t][:, S:], 0.0)
         nc.vector.memset(h_all[:, PACK * S :], 0.0)
-        nc.vector.memset(half_col[:], 0.5)
 
+        warm_sigmoid = sbt("warm_sigmoid", [P, 1], F32)
+        nc.scalar.activation(out=warm_sigmoid[:], in_=half_col[:], func=ACT.Sigmoid)
         ds_got = sbt("ds_got", [P, H], U8, tag="ds_got_then_w")
         nc.vector.tensor_copy(out=ds_got[:], in_=ds_win[:].indirect(k1_l[:]))
         ds_dealt = sbt("ds_dealt", [P, H], U8, tag="ds_dealt_then_ws")
@@ -199,6 +201,9 @@ def tile_picked_kjgclipgmaxfrac_none_po_kernel(
                 nc.scalar.activation(
                     out=other[:, t * HALF : (t + 1) * HALF], in_=b_win[t][:].indirect(n3_l[:, ls]), func=ACT.Copy
                 )
+            if u == 1:
+                warm_ln = sbt("warm_ln", [P, 1], F32)
+                nc.scalar.activation(out=warm_ln[:], in_=other[:, PACK * HALF - 1 :], func=ACT.Ln, bias=half_col[:], scale=0.0)
             gated = sbt(f"gated{u}", [P, PACK, HALF], F32)
             for v in range(2):
                 nc.vector.scalar_tensor_tensor(

@@ -17,7 +17,7 @@ PACK = 4
 T, G, S, H, MEMBERS = 1024, 2048, 256, 512, 4
 HALF = S // 2
 QUART = S // 4
-A_WIN = 528
+A_WIN = 1040
 B_WIN = 512
 FLOPS = 2 * 512 * 512 * 256 * 4
 
@@ -29,6 +29,12 @@ def words_of(dram):
 def deal(nc, dst, src):
     nc.vector.tensor_copy(
         out=dst.rearrange("p (t m) -> p m t", t=PACK), in_=src.rearrange("p (m t) -> p m t", t=PACK)
+    )
+
+
+def deal_bytes(nc, dst, src):
+    nc.vector.tensor_copy(
+        out=dst.rearrange("p (t m) -> p t m", t=PACK), in_=src.rearrange("p (m t) -> p t m", t=PACK)
     )
 
 
@@ -58,31 +64,28 @@ def tile_picked_kjgclipgmaxfrac_none_po_kernel(
         def sbt(name, shape, dtype, tag=None):
             return sb.tile(shape, dtype, name=name, tag=tag or name, align_bytes=64)
 
-        d_win = sbt("d_win", [P, G], U32)
+        d_win = sbt("d_win", [P, G], U32, tag="d_win_then_w")
         x_win = sbt("x_win", [P, T], U32)
         ds_win = sbt("ds_win", [P, G], U8)
         xs_win = sbt("xs_win", [P, T], U8)
-        ds_plane = sbt("ds_plane", [P, H], U8)
+        s_moved = sbt("s_moved", [P, H + 2 * S], U8)
         a_win = [sbt(f"a_win{t}", [P, A_WIN], F32) for t in range(PACK)]
         b_win = [sbt(f"b_win{t}", [P, B_WIN], F32) for t in range(PACK)]
         h_all = sbt("h_all", [P, (PACK + 1) * S], F32)
         half_col = sbt("half_col", [P, 1], F32)
 
         nc.vector.memset(half_col[:], 0.5)
-        nc.vector.memset(ds_plane[:].bitcast(I32), 0)
+        nc.vector.memset(s_moved[:].bitcast(I32), 0)
 
-        nc.scalar.dma_start(d_win[:].bitcast(I32), words_of(d_words))
         k1_l = list_tile("k1_l", k1)
-        nc.scalar.dma_start(x_win[:].bitcast(I32), words_of(x_words))
         nc.sync.dma_start(ds_win[:].bitcast(I32), d_scales[0].bitcast(I32).unsqueeze(1).to_broadcast([16, 8, G // 4]))
         offs_l = list_tile("offs_l", offs)
-        for q in range(4):
-            rows = x_scales[0, 4 * q : 4 * q + 4, :].bitcast(I32)
-            eng = nc.sync if q == 0 else nc.gpsimd
-            eng.dma_start(xs_win[32 * q : 32 * q + 32, :].bitcast(I32), rows.unsqueeze(0).to_broadcast([8, 4, T // 4]))
+        nc.sync.dma_start(xs_win[:].bitcast(I32), x_scales[0].bitcast(I32).unsqueeze(1).to_broadcast([16, 8, T // 4]))
         two_l = list_tile("two_l", two)
         n1_l = list_tile("n1_l", n1)
         n2_l = list_tile("n2_l", n2)
+        nc.sync.dma_start(d_win[:].bitcast(I32), words_of(d_words))
+        nc.sync.dma_start(x_win[:].bitcast(I32), words_of(x_words))
         n3_l = list_tile("n3_l", n3)
         n4_l = list_tile("n4_l", n4)
         n5_l = list_tile("n5_l", n5)
@@ -91,48 +94,45 @@ def tile_picked_kjgclipgmaxfrac_none_po_kernel(
         nc.gpsimd.dma_start(gn_t[:], gn.rearrange("(p t) o -> p (t o)", t=PACK))
         nc.gpsimd.dma_start(gm_t[:], gm.rearrange("(p t) o -> p (t o)", t=PACK))
 
-        for t in range(PACK):
-            nc.vector.memset(a_win[t][:, S:], 0.0)
-        for t in range(PACK):
-            nc.vector.memset(b_win[t][:, S:], 0.0)
-        nc.vector.memset(h_all[:, PACK * S :], 0.0)
-
         warm_sigmoid = sbt("warm_sigmoid", [P, 1], F32)
         nc.scalar.activation(out=warm_sigmoid[:], in_=half_col[:], func=ACT.Sigmoid)
-        ds_got = sbt("ds_got", [P, H], U8, tag="ds_got_then_w")
-        nc.vector.tensor_copy(out=ds_got[:], in_=ds_win[:].indirect(k1_l[:]))
-        ds_dealt = sbt("ds_dealt", [P, H], U8, tag="ds_dealt_then_ws")
-        deal(nc, ds_dealt[:], ds_got[:])
+        s_got = sbt("s_got", [P, H + 2 * S], U8)
+        nc.vector.tensor_copy(out=s_got[:, :H], in_=ds_win[:].indirect(k1_l[:]))
+        nc.vector.tensor_copy(out=s_got[:, H : H + S], in_=xs_win[:].indirect(offs_l[:]))
+        nc.vector.tensor_copy(out=s_got[:, H + S :], in_=xs_win[:].indirect(two_l[:]))
         for b in range(4):
-            nc.scalar.dma_start(ds_plane[b:P:32, :].bitcast(I32), ds_dealt[8 * b : P : 32, :].bitcast(I32))
-        w_raw = sbt("w_raw", [P, 2 * H], U32, tag="ds_got_then_w")
+            nc.scalar.dma_start(s_moved[b:P:32, :].bitcast(I32), s_got[8 * b : P : 32, :].bitcast(I32))
+        xa_s = s_moved[:, H : H + S]
+        xb_s = s_moved[:, H + S :]
+
+        xa_w = sbt("xa_w", [P, S], U32)
+        xb_w = sbt("xb_w", [P, S], U32)
+        d_got = sbt("d_got", [P, H], U32, tag="d_got_then_ws")
+        d_dealt = sbt("d_dealt", [P, H], U32)
+        nc.vector.tensor_copy(out=d_got[:], in_=d_win[:].indirect(k1_l[:]))
+        deal(nc, d_dealt[:].bitcast(I32), d_got[:].bitcast(I32))
+        nc.vector.tensor_copy(out=xa_w[:], in_=x_win[:].indirect(offs_l[:]))
+        ds_plane = sbt("ds_plane", [P, H], U8)
+        deal_bytes(nc, ds_plane[:], s_moved[:, :H])
+        nc.vector.tensor_copy(out=xb_w[:], in_=x_win[:].indirect(two_l[:]))
+
+        w_raw = sbt("w_raw", [P, 2 * H], U32, tag="d_win_then_w")
         nc.sync.dma_start(w_raw[:, :H].bitcast(I32), words_of(w1_words))
         nc.sync.dma_start(w_raw[:, H:].bitcast(I32), words_of(w2_words))
-        ws_raw = sbt("ws_raw", [P, H], U8, tag="ds_dealt_then_ws")
+        ws_raw = sbt("ws_raw", [P, H], U8, tag="d_got_then_ws")
         nc.gpsimd.memset(ws_raw[:].bitcast(I32), 0)
         for k, scales in enumerate((w1_scales, w2_scales)):
             for q in range(4):
                 r0 = 32 * q + 4 * k
                 nc.sync.dma_start(ws_raw[r0 : r0 + 4, :].bitcast(I32), scales[0, 4 * q : 4 * q + 4, :].bitcast(I32))
-
-        xb_s = sbt("xb_s", [P, S], U8)
-        xa_w = sbt("xa_w", [P, S], U32)
-        xb_w = sbt("xb_w", [P, S], U32)
-        d_got = sbt("d_got", [P, H], U32, tag="d_got_then_xa_s")
-        d_dealt = sbt("d_dealt", [P, H], U32)
-        nc.vector.tensor_copy(out=d_got[:], in_=d_win[:].indirect(k1_l[:]))
-        deal(nc, d_dealt[:].bitcast(I32), d_got[:].bitcast(I32))
-        xa_s = sbt("xa_s", [P, S], U8, tag="d_got_then_xa_s")
-        nc.vector.tensor_copy(out=xa_s[:], in_=xs_win[:].indirect(offs_l[:]))
-        nc.vector.tensor_copy(out=xa_w[:], in_=x_win[:].indirect(offs_l[:]))
         gn16 = sbt("gn16", [P, PACK], F32)
-        nc.vector.tensor_scalar(out=gn16[:], in0=gn_t[:], scalar1=0.0625, scalar2=None, op0=ALU.mult)
+        nc.gpsimd.tensor_scalar(out=gn16[:], in0=gn_t[:], scalar1=0.0625, scalar2=0.0, op0=ALU.mult, op1=ALU.add)
 
         def score(out, t, xw, xs):
             cols = slice(t * P, (t + 1) * P)
             nc.tensor.matmul_mx(
                 out=out, lhsT=d_dealt[:, cols].bitcast(FP8X4), lhsT_scale=ds_plane[:, cols],
-                rhs=xw[:].bitcast(FP8X4), rhs_scale=xs[:], start=True, stop=True,
+                rhs=xw[:].bitcast(FP8X4), rhs_scale=xs, start=True, stop=True,
             )
 
         a_ps0 = ps.tile([P, S], F32, name="a_ps0")
@@ -141,14 +141,17 @@ def tile_picked_kjgclipgmaxfrac_none_po_kernel(
         a_ps = [a_ps0[:], a_ps1[:], a_ps23[:, 0, :], a_ps23[:, 1, :]]
         for t in range(PACK):
             score(a_ps[t], t, xa_w, xa_s)
-        for t in range(PACK):
-            nc.scalar.activation(out=a_win[t][:, :S], in_=a_ps[t], func=ACT.Copy, scale=gn16[:, t : t + 1])
+        nc.scalar.activation(out=a_win[0][:, :S], in_=a_ps[0], func=ACT.Copy, scale=gn16[:, 0:1])
+        for t in range(1, PACK):
+            nc.vector.tensor_scalar(out=a_win[t][:, :S], in0=a_ps[t], scalar1=gn16[:, t : t + 1], scalar2=None, op0=ALU.mult)
 
-        nc.vector.tensor_copy(out=xb_w[:], in_=x_win[:].indirect(two_l[:]))
-        nc.vector.tensor_copy(out=xb_s[:], in_=xs_win[:].indirect(two_l[:]))
         b_ps = [ps.tile([P, 2, S], F32, name=f"b_ps{u}") for u in range(2)]
         for t in range(PACK):
             score(b_ps[t // 2][:, t % 2, :], t, xb_w, xb_s)
+        for t in range(PACK):
+            nc.vector.tensor_scalar(
+                out=b_win[t][:, :S], in0=b_ps[t // 2][:, t % 2, :], scalar1=0.0625, scalar2=None, op0=ALU.mult
+            )
 
         w_dealt = sbt("w_dealt", [P, 2 * H], U32)
         ws_plane = sbt("ws_plane", [P, H], U8)
@@ -158,31 +161,38 @@ def tile_picked_kjgclipgmaxfrac_none_po_kernel(
         capped = sbt("capped", [P, PACK * S], F32)
         for t in range(PACK):
             mb = sbt(f"mb{t}", [P, MEMBERS * S], F32)
-            for u in range(2):
-                nc.scalar.activation(
-                    out=mb[:, u * 512 : (u + 1) * 512], in_=a_win[t][:].indirect(n1_l[:, u * 32 : (u + 1) * 32]), func=ACT.Copy
-                )
             pairs = mb[:].rearrange("p (j u e) -> p j u e", u=2, e=2)
             hi = sbt(f"hi{t}", [P, S, 2], F32)
             lo = sbt(f"lo{t}", [P, S, 2], F32)
             upper = sbt(f"upper{t}", [P, S], F32)
             cols = slice(t * S, (t + 1) * S)
-            nc.vector.tensor_tensor(out=hi[:], in0=pairs[:, :, 0, :], in1=pairs[:, :, 1, :], op=ALU.max)
-            nc.vector.tensor_tensor(out=lo[:], in0=pairs[:, :, 0, :], in1=pairs[:, :, 1, :], op=ALU.min)
+            for js in [slice(0, HALF), slice(HALF, S)] if t in (0, PACK - 1) else [slice(0, S)]:
+                entries = slice(js.start * MEMBERS, js.stop * MEMBERS)
+                offsets = n1_l[:, entries.start // 16 : entries.stop // 16]
+                nc.scalar.activation(out=mb[:, entries], in_=a_win[t][:].indirect(offsets), func=ACT.Copy)
+                nc.vector.tensor_tensor(out=hi[:, js], in0=pairs[:, js, 0, :], in1=pairs[:, js, 1, :], op=ALU.max)
+                nc.vector.tensor_tensor(out=lo[:, js], in0=pairs[:, js, 0, :], in1=pairs[:, js, 1, :], op=ALU.min)
             nc.vector.tensor_tensor(out=upper[:], in0=hi[:, :, 0], in1=hi[:, :, 1], op=ALU.max)
             nc.vector.tensor_tensor(out=lower[:, cols], in0=lo[:, :, 0], in1=lo[:, :, 1], op=ALU.min)
             nc.vector.scalar_tensor_tensor(
                 out=capped[:, cols], in0=a_win[t][:, :S], scalar=1.5, in1=upper[:], op0=ALU.mult, op1=ALU.min
             )
-        deal(nc, ws_plane[:], ws_raw[:])
+        deal_bytes(nc, ws_plane[:], ws_raw[:])
         z_bf = sbt("z_bf", [P, S * PACK], BF16)
         nc.vector.tensor_tensor(out=walk_dst(z_bf[:]), in0=walk_src(capped[:]), in1=walk_src(lower[:]), op=ALU.max)
         z_codes = sbt("z_codes", [P, S], U32)
         z_plane = sbt("z_plane", [P, S], U8)
         nc.vector.quantize_mx(out=z_codes[:].bitcast(FP8X4), scales=z_plane[:], in_=z_bf[:])
 
+        gate = sbt("gate", [P, PACK, S], F32)
+        gated = sbt("gated", [P, PACK, S], F32)
         for t in range(PACK):
-            nc.scalar.activation(out=b_win[t][:, :S], in_=b_ps[t // 2][:, t % 2, :], func=ACT.Copy, scale=0.0625)
+            nc.scalar.activation(out=gate[:, t, :], in_=b_win[t][:].indirect(n2_l[:]), func=ACT.Sigmoid)
+        for v in range(2):
+            nc.vector.scalar_tensor_tensor(
+                out=gated[:, 2 * v : 2 * v + 2, :], in0=b_ps[v][:], scalar=0.0625,
+                in1=gate[:, 2 * v : 2 * v + 2, :], op0=ALU.mult, op1=ALU.mult,
+            )
 
         h_view = h_all[:, : PACK * S].rearrange("p (t j) -> p t j", t=PACK)
         h_ps = [
@@ -193,10 +203,7 @@ def tile_picked_kjgclipgmaxfrac_none_po_kernel(
         for u in range(2):
             js = slice(u * HALF, (u + 1) * HALF)
             ls = slice(u * HALF // 16, (u + 1) * HALF // 16)
-            gate = sbt(f"gate{u}", [P, PACK, HALF], F32)
             other = sbt(f"other{u}", [P, PACK * HALF], F32)
-            for t in range(PACK):
-                nc.scalar.activation(out=gate[:, t, :], in_=b_win[t][:].indirect(n2_l[:, ls]), func=ACT.Sigmoid)
             for t in range(PACK):
                 nc.scalar.activation(
                     out=other[:, t * HALF : (t + 1) * HALF], in_=b_win[t][:].indirect(n3_l[:, ls]), func=ACT.Copy
@@ -204,16 +211,13 @@ def tile_picked_kjgclipgmaxfrac_none_po_kernel(
             if u == 1:
                 warm_ln = sbt("warm_ln", [P, 1], F32)
                 nc.scalar.activation(out=warm_ln[:], in_=other[:, PACK * HALF - 1 :], func=ACT.Ln, bias=half_col[:], scale=0.0)
-            gated = sbt(f"gated{u}", [P, PACK, HALF], F32)
-            for v in range(2):
-                nc.vector.scalar_tensor_tensor(
-                    out=gated[:, 2 * v : 2 * v + 2, :], in0=b_ps[v][:, :, js], scalar=0.0625,
-                    in1=gate[:, 2 * v : 2 * v + 2, :], op0=ALU.mult, op1=ALU.mult,
-                )
             larger = sbt(f"larger{u}", [P, PACK * HALF], F32)
-            gated_flat = gated[:].rearrange("p t j -> p (t j)")
-            for c in (slice(0, 3 * HALF), slice(3 * HALF, 4 * HALF)):
-                nc.vector.tensor_tensor(out=larger[:, c], in0=gated_flat[:, c], in1=other[:, c], op=ALU.max)
+            for ts in (slice(0, 3), slice(3, 4)):
+                c = slice(ts.start * HALF, ts.stop * HALF)
+                nc.vector.tensor_tensor(
+                    out=larger[:, c].rearrange("p (t j) -> p t j", j=HALF), in0=gated[:, ts, js],
+                    in1=other[:, c].rearrange("p (t j) -> p t j", j=HALF), op=ALU.max,
+                )
             z2_bf = sbt(f"z2_bf{u}", [P, HALF * PACK], BF16)
             nc.vector.tensor_tensor(out=walk_dst(z2_bf[:]), in0=walk_src(larger[:]), in1=gm_b, op=ALU.mult)
             z2_codes = sbt(f"z2_codes{u}", [P, HALF], U32)
@@ -229,14 +233,14 @@ def tile_picked_kjgclipgmaxfrac_none_po_kernel(
                         rhs=codes.bitcast(FP8X4), rhs_scale=plane,
                         start=(k == 0 and t % per_bank == 0), stop=(k == 1 and t % per_bank == per_bank - 1),
                     )
-            if u == 0:
-                nc.scalar.copy(out=h_view[:, :, js], in_=h_ps[0][0][:])
-            else:
-                nc.scalar.copy(out=h_view[:, 0:2, js], in_=h_ps[1][0][:])
-                nc.vector.tensor_copy(out=h_view[:, 2:4, js], in_=h_ps[1][1][:])
+        nc.scalar.copy(out=h_view[:, :, :HALF], in_=h_ps[0][0][:])
+        nc.scalar.copy(out=h_view[:, 0:2, HALF:], in_=h_ps[1][0][:])
+        nc.vector.tensor_copy(out=h_view[:, 2:4, HALF:], in_=h_ps[1][1][:])
 
-        far, near, numer, y = [sbt(n, [P, PACK, S], F32) for n in ("far", "near", "numer", "y")]
-        diff, dist, logs = [sbt(n, [P, 4, PACK, QUART], F32) for n in ("diff", "dist", "logs")]
+        far = sbt("far", [P, PACK, S], F32, tag="far_then_numer")
+        y = sbt("y", [P, PACK, S], F32)
+        diff = sbt("diff", [P, 4, PACK, QUART], F32, tag="diff_then_near")
+        dist, logs = [sbt(n, [P, 4, PACK, QUART], F32) for n in ("dist", "logs")]
         pieces = [slice(0, 2), slice(2, 3), slice(3, 4)]
 
         def cols_of(qs, width):
@@ -256,28 +260,37 @@ def tile_picked_kjgclipgmaxfrac_none_po_kernel(
             nc.vector.tensor_tensor(
                 out=diff[:, qs], in0=by_quarter(far[:, :, js]), in1=by_quarter(h_view[:, :, js]), op=ALU.subtract
             )
-            nc.vector.scalar_tensor_tensor(
-                out=flat(dist[:, qs]), in0=flat(diff[:, qs]), scalar=-1.0, in1=flat(diff[:, qs]), op0=ALU.mult, op1=ALU.max
-            )
+            if qs.stop == 4:
+                nc.scalar.activation(out=flat(dist[:, qs]), in_=flat(diff[:, qs]), func=ACT.Abs)
+            else:
+                nc.vector.scalar_tensor_tensor(
+                    out=flat(dist[:, qs]), in0=flat(diff[:, qs]), scalar=-1.0, in1=flat(diff[:, qs]), op0=ALU.mult, op1=ALU.max
+                )
         for qs in pieces:
             nc.scalar.activation(out=flat(logs[:, qs]), in_=flat(dist[:, qs]), func=ACT.Ln, bias=half_col[:])
+        numer = sbt("numer", [P, PACK, S], F32, tag="far_then_numer")
         for u in range(2):
             js = slice(u * HALF, (u + 1) * HALF)
             ls = slice(u * HALF // 16, (u + 1) * HALF // 16)
+            near = sbt(f"near{u}", [P, PACK, HALF], F32, tag="diff_then_near" if u else None)
             for t in range(PACK):
-                nc.vector.tensor_copy(out=near[:, t, js], in_=h_all[:, t * S : (t + 2) * S].indirect(n4_l[:, ls]))
-            nc.vector.tensor_tensor(out=numer[:, :, js], in0=h_view[:, :, js], in1=near[:, :, js], op=ALU.subtract)
+                nc.vector.tensor_copy(out=near[:, t, :], in_=h_all[:, t * S : (t + 2) * S].indirect(n4_l[:, ls]))
+            nc.vector.tensor_tensor(out=numer[:, :, js], in0=h_view[:, :, js], in1=near[:], op=ALU.subtract)
         y_codes = sbt("y_codes", [P, S], U32)
         y_plane = sbt("y_plane", [P, S], U8)
         y_bf = sbt("y_bf", [P, S * PACK], BF16)
         out_view = out_0.rearrange("(p t) j -> p t j", t=PACK)
         recip = dist[:].rearrange("p t q c -> p t (q c)")
-        for qs in pieces:
+        for qs in [slice(q, q + 1) for q in range(4)]:
             js = cols_of(qs, QUART)
             nc.scalar.activation(out=by_quarter(recip[:, :, js]), in_=logs[:, qs], func=ACT.Exp, scale=-1.0)
             nc.vector.tensor_tensor(out=y[:, :, js], in0=numer[:, :, js], in1=recip[:, :, js], op=ALU.mult)
             bf = y_bf[:, cols_of(qs, QUART * PACK)]
-            nc.vector.tensor_copy(out=walk_dst(bf), in_=y[:, :, js].rearrange("p t (c i) -> p c t i", i=4))
+            y_walk = y[:, :, js].rearrange("p t (c i) -> p c t i", i=4)
+            if qs.start < 2:
+                nc.scalar.copy(out=walk_dst(bf), in_=y_walk)
+            else:
+                nc.vector.tensor_copy(out=walk_dst(bf), in_=y_walk)
             nc.vector.quantize_mx(out=y_codes[:, js].bitcast(FP8X4), scales=y_plane[:, js], in_=bf)
             if qs.stop % 2 == 0:
                 hs = slice(js.stop - HALF, js.stop)

from contextlib import ExitStack

import concourse.mybir as mybir

F32 = mybir.dt.float32
BF16 = mybir.dt.bfloat16
I32 = mybir.dt.int32
U32 = mybir.dt.uint32
U16 = mybir.dt.uint16
U8 = mybir.dt.uint8
FP8X4 = mybir.dt.float8_e4m3fn_x4
ALU = mybir.AluOpType
ACT = mybir.ActivationFunctionType

P = 128
PACK = 4
T, G, S, H, MEMBERS = 1024, 2048, 256, 512, 4
HALF = S // 2
QUART = S // 4
A_WIN = 1040
B_WIN = 512
FLOPS = 2 * 512 * 512 * 256 * 4


def words_of(dram):
    return dram[0].rearrange("p n t -> p (n t)").bitcast(I32)


def deal(nc, dst, src):
    nc.vector.tensor_copy(
        out=dst.rearrange("p (t m) -> p m t", t=PACK), in_=src.rearrange("p (m t) -> p m t", t=PACK)
    )


def deal_bytes(nc, dst, src):
    nc.vector.tensor_copy(
        out=dst.rearrange("p (t m) -> p t m", t=PACK), in_=src.rearrange("p (m t) -> p t m", t=PACK)
    )


def walk_src(ap):
    return ap.rearrange("p (t c i) -> p c t i", t=PACK, i=4)


def walk_dst(ap):
    return ap.rearrange("p (c i t) -> p c t i", t=PACK, i=4)


def tile_picked_kjgclipgmaxfrac_none_po_kernel(
    tc, x_words, x_scales, d_words, d_scales, gn, gm, w1_words, w1_scales, w2_words, w2_scales,
    offs, k1, two, n1, n2, n3, n4, n5, out_0, out_1, out_2,
):
    nc = tc.nc
    with ExitStack() as ctx:
        lists = ctx.enter_context(tc.tile_pool(name="lists", bufs=1))
        sb = ctx.enter_context(tc.tile_pool(name="sb", bufs=1))
        ps = ctx.enter_context(tc.psum_pool(name="ps", bufs=1))

        def list_tile(name, dram):
            tl = lists.tile(list(dram.shape), U16, name=name)
            nc.sync.dma_start(tl[:], dram)
            return tl

        def sbt(name, shape, dtype, tag=None):
            return sb.tile(shape, dtype, name=name, tag=tag or name, align_bytes=64)

        d_win = sbt("d_win", [P, G], U32, tag="d_win_then_w")
        x_win = sbt("x_win", [P, T], U32)
        ds_win = sbt("ds_win", [P, G], U8)
        xs_win = sbt("xs_win", [P, T], U8)
        s_moved = sbt("s_moved", [P, H + 2 * S], U8)
        a_win = [sbt(f"a_win{t}", [P, A_WIN], F32) for t in range(PACK)]
        b_win = [sbt(f"b_win{t}", [P, B_WIN], F32) for t in range(PACK)]
        h_all = sbt("h_all", [P, (PACK + 1) * S], F32)
        half_col = sbt("half_col", [P, 1], F32)

        nc.vector.memset(half_col[:], 0.5)
        nc.vector.memset(s_moved[:].bitcast(I32), 0)

        k1_l = list_tile("k1_l", k1)
        nc.sync.dma_start(ds_win[:].bitcast(I32), d_scales[0].bitcast(I32).unsqueeze(1).to_broadcast([16, 8, G // 4]))
        offs_l = list_tile("offs_l", offs)
        nc.sync.dma_start(xs_win[:].bitcast(I32), x_scales[0].bitcast(I32).unsqueeze(1).to_broadcast([16, 8, T // 4]))
        two_l = list_tile("two_l", two)
        n1_l = list_tile("n1_l", n1)
        n2_l = list_tile("n2_l", n2)
        nc.sync.dma_start(d_win[:].bitcast(I32), words_of(d_words))
        nc.sync.dma_start(x_win[:].bitcast(I32), words_of(x_words))
        n3_l = list_tile("n3_l", n3)
        n4_l = list_tile("n4_l", n4)
        n5_l = list_tile("n5_l", n5)
        gn_t = sbt("gn_t", [P, PACK], F32)
        gm_t = sbt("gm_t", [P, PACK], F32)
        nc.gpsimd.dma_start(gn_t[:], gn.rearrange("(p t) o -> p (t o)", t=PACK))
        nc.gpsimd.dma_start(gm_t[:], gm.rearrange("(p t) o -> p (t o)", t=PACK))

        warm_sigmoid = sbt("warm_sigmoid", [P, 1], F32)
        nc.scalar.activation(out=warm_sigmoid[:], in_=half_col[:], func=ACT.Sigmoid)
        s_got = sbt("s_got", [P, H + 2 * S], U8)
        nc.vector.tensor_copy(out=s_got[:, :H], in_=ds_win[:].indirect(k1_l[:]))
        nc.vector.tensor_copy(out=s_got[:, H : H + S], in_=xs_win[:].indirect(offs_l[:]))
        nc.vector.tensor_copy(out=s_got[:, H + S :], in_=xs_win[:].indirect(two_l[:]))
        for b in range(4):
            nc.scalar.dma_start(s_moved[b:P:32, :].bitcast(I32), s_got[8 * b : P : 32, :].bitcast(I32))
        xa_s = s_moved[:, H : H + S]
        xb_s = s_moved[:, H + S :]

        xa_w = sbt("xa_w", [P, S], U32)
        xb_w = sbt("xb_w", [P, S], U32)
        d_got = sbt("d_got", [P, H], U32, tag="d_got_then_ws")
        d_dealt = sbt("d_dealt", [P, H], U32)
        nc.vector.tensor_copy(out=d_got[:], in_=d_win[:].indirect(k1_l[:]))
        deal(nc, d_dealt[:].bitcast(I32), d_got[:].bitcast(I32))
        nc.vector.tensor_copy(out=xa_w[:], in_=x_win[:].indirect(offs_l[:]))
        ds_plane = sbt("ds_plane", [P, H], U8)
        deal_bytes(nc, ds_plane[:], s_moved[:, :H])
        nc.vector.tensor_copy(out=xb_w[:], in_=x_win[:].indirect(two_l[:]))

        w_raw = sbt("w_raw", [P, 2 * H], U32, tag="d_win_then_w")
        nc.sync.dma_start(w_raw[:, :H].bitcast(I32), words_of(w1_words))
        nc.sync.dma_start(w_raw[:, H:].bitcast(I32), words_of(w2_words))
        ws_raw = sbt("ws_raw", [P, H], U8, tag="d_got_then_ws")
        nc.gpsimd.memset(ws_raw[:].bitcast(I32), 0)
        for k, scales in enumerate((w1_scales, w2_scales)):
            for q in range(4):
                r0 = 32 * q + 4 * k
                nc.sync.dma_start(ws_raw[r0 : r0 + 4, :].bitcast(I32), scales[0, 4 * q : 4 * q + 4, :].bitcast(I32))
        gn16 = sbt("gn16", [P, PACK], F32)
        nc.gpsimd.tensor_scalar(out=gn16[:], in0=gn_t[:], scalar1=0.0625, scalar2=0.0, op0=ALU.mult, op1=ALU.add)

        def score(out, t, xw, xs):
            cols = slice(t * P, (t + 1) * P)
            nc.tensor.matmul_mx(
                out=out, lhsT=d_dealt[:, cols].bitcast(FP8X4), lhsT_scale=ds_plane[:, cols],
                rhs=xw[:].bitcast(FP8X4), rhs_scale=xs, start=True, stop=True,
            )

        a_ps0 = ps.tile([P, S], F32, name="a_ps0")
        a_ps1 = ps.tile([P, S], F32, name="a_ps1")
        a_ps23 = ps.tile([P, 2, S], F32, name="a_ps23")
        a_ps = [a_ps0[:], a_ps1[:], a_ps23[:, 0, :], a_ps23[:, 1, :]]
        for t in range(PACK):
            score(a_ps[t], t, xa_w, xa_s)
        nc.scalar.activation(out=a_win[0][:, :S], in_=a_ps[0], func=ACT.Copy, scale=gn16[:, 0:1])
        for t in range(1, PACK):
            nc.vector.tensor_scalar(out=a_win[t][:, :S], in0=a_ps[t], scalar1=gn16[:, t : t + 1], scalar2=None, op0=ALU.mult)

        b_ps = [ps.tile([P, 2, S], F32, name=f"b_ps{u}") for u in range(2)]
        for t in range(PACK):
            score(b_ps[t // 2][:, t % 2, :], t, xb_w, xb_s)
        for t in range(PACK):
            nc.vector.tensor_scalar(
                out=b_win[t][:, :S], in0=b_ps[t // 2][:, t % 2, :], scalar1=0.0625, scalar2=None, op0=ALU.mult
            )

        w_dealt = sbt("w_dealt", [P, 2 * H], U32)
        ws_plane = sbt("ws_plane", [P, H], U8)
        for k in range(2):
            deal(nc, w_dealt[:, k * H : (k + 1) * H].bitcast(I32), w_raw[:, k * H : (k + 1) * H].bitcast(I32))
        lower = sbt("lower", [P, PACK * S], F32)
        capped = sbt("capped", [P, PACK * S], F32)
        for t in range(PACK):
            mb = sbt(f"mb{t}", [P, MEMBERS * S], F32)
            pairs = mb[:].rearrange("p (j u e) -> p j u e", u=2, e=2)
            hi = sbt(f"hi{t}", [P, S, 2], F32)
            lo = sbt(f"lo{t}", [P, S, 2], F32)
            upper = sbt(f"upper{t}", [P, S], F32)
            cols = slice(t * S, (t + 1) * S)
            for js in [slice(0, HALF), slice(HALF, S)] if t in (0, PACK - 1) else [slice(0, S)]:
                entries = slice(js.start * MEMBERS, js.stop * MEMBERS)
                offsets = n1_l[:, entries.start // 16 : entries.stop // 16]
                nc.scalar.activation(out=mb[:, entries], in_=a_win[t][:].indirect(offsets), func=ACT.Copy)
                nc.vector.tensor_tensor(out=hi[:, js], in0=pairs[:, js, 0, :], in1=pairs[:, js, 1, :], op=ALU.max)
                nc.vector.tensor_tensor(out=lo[:, js], in0=pairs[:, js, 0, :], in1=pairs[:, js, 1, :], op=ALU.min)
            nc.vector.tensor_tensor(out=upper[:], in0=hi[:, :, 0], in1=hi[:, :, 1], op=ALU.max)
            nc.vector.tensor_tensor(out=lower[:, cols], in0=lo[:, :, 0], in1=lo[:, :, 1], op=ALU.min)
            nc.vector.scalar_tensor_tensor(
                out=capped[:, cols], in0=a_win[t][:, :S], scalar=1.5, in1=upper[:], op0=ALU.mult, op1=ALU.min
            )
        deal_bytes(nc, ws_plane[:], ws_raw[:])
        z_bf = sbt("z_bf", [P, S * PACK], BF16)
        nc.vector.tensor_tensor(out=walk_dst(z_bf[:]), in0=walk_src(capped[:]), in1=walk_src(lower[:]), op=ALU.max)
        z_codes = sbt("z_codes", [P, S], U32)
        z_plane = sbt("z_plane", [P, S], U8)
        nc.vector.quantize_mx(out=z_codes[:].bitcast(FP8X4), scales=z_plane[:], in_=z_bf[:])

        gate = sbt("gate", [P, PACK, S], F32)
        gated = sbt("gated", [P, PACK, S], F32)
        for t in range(PACK):
            nc.scalar.activation(out=gate[:, t, :], in_=b_win[t][:].indirect(n2_l[:]), func=ACT.Sigmoid)
        for v in range(2):
            nc.vector.scalar_tensor_tensor(
                out=gated[:, 2 * v : 2 * v + 2, :], in0=b_ps[v][:], scalar=0.0625,
                in1=gate[:, 2 * v : 2 * v + 2, :], op0=ALU.mult, op1=ALU.mult,
            )

        h_view = h_all[:, : PACK * S].rearrange("p (t j) -> p t j", t=PACK)
        h_ps = [
            [ps.tile([P, PACK, HALF], F32, name="h_ps0")],
            [ps.tile([P, 2, HALF], F32, name="h_ps1a"), ps.tile([P, 2, HALF], F32, name="h_ps1b")],
        ]
        gm_b = gm_t[:].unsqueeze(1).unsqueeze(3).to_broadcast([P, HALF // 4, PACK, 4])
        for u in range(2):
            js = slice(u * HALF, (u + 1) * HALF)
            ls = slice(u * HALF // 16, (u + 1) * HALF // 16)
            other = sbt(f"other{u}", [P, PACK * HALF], F32)
            for t in range(PACK):
                nc.scalar.activation(
                    out=other[:, t * HALF : (t + 1) * HALF], in_=b_win[t][:].indirect(n3_l[:, ls]), func=ACT.Copy
                )
            if u == 1:
                warm_ln = sbt("warm_ln", [P, 1], F32)
                nc.scalar.activation(out=warm_ln[:], in_=other[:, PACK * HALF - 1 :], func=ACT.Ln, bias=half_col[:], scale=0.0)
            larger = sbt(f"larger{u}", [P, PACK * HALF], F32)
            for ts in (slice(0, 3), slice(3, 4)):
                c = slice(ts.start * HALF, ts.stop * HALF)
                nc.vector.tensor_tensor(
                    out=larger[:, c].rearrange("p (t j) -> p t j", j=HALF), in0=gated[:, ts, js],
                    in1=other[:, c].rearrange("p (t j) -> p t j", j=HALF), op=ALU.max,
                )
            z2_bf = sbt(f"z2_bf{u}", [P, HALF * PACK], BF16)
            nc.vector.tensor_tensor(out=walk_dst(z2_bf[:]), in0=walk_src(larger[:]), in1=gm_b, op=ALU.mult)
            z2_codes = sbt(f"z2_codes{u}", [P, HALF], U32)
            z2_plane = sbt(f"z2_plane{u}", [P, HALF], U8)
            nc.vector.quantize_mx(out=z2_codes[:].bitcast(FP8X4), scales=z2_plane[:], in_=z2_bf[:])
            per_bank = PACK // len(h_ps[u])
            for k, (codes, plane) in enumerate(((z_codes[:, js], z_plane[:, js]), (z2_codes[:], z2_plane[:]))):
                for t in range(PACK):
                    nc.tensor.matmul_mx(
                        out=h_ps[u][t // per_bank][:, t % per_bank, :],
                        lhsT=w_dealt[:, k * H + t * P : k * H + (t + 1) * P].bitcast(FP8X4),
                        lhsT_scale=ws_plane[4 * k : P, t * P : (t + 1) * P],
                        rhs=codes.bitcast(FP8X4), rhs_scale=plane,
                        start=(k == 0 and t % per_bank == 0), stop=(k == 1 and t % per_bank == per_bank - 1),
                    )
        nc.scalar.copy(out=h_view[:, :, :HALF], in_=h_ps[0][0][:])
        nc.scalar.copy(out=h_view[:, 0:2, HALF:], in_=h_ps[1][0][:])
        nc.vector.tensor_copy(out=h_view[:, 2:4, HALF:], in_=h_ps[1][1][:])

        far = sbt("far", [P, PACK, S], F32, tag="far_then_numer")
        y = sbt("y", [P, PACK, S], F32)
        diff = sbt("diff", [P, 4, PACK, QUART], F32, tag="diff_then_near")
        dist, logs = [sbt(n, [P, 4, PACK, QUART], F32) for n in ("dist", "logs")]
        pieces = [slice(0, 2), slice(2, 3), slice(3, 4)]

        def cols_of(qs, width):
            return slice(qs.start * width, qs.stop * width)

        def by_quarter(ap):
            return ap.rearrange("p t (q c) -> p q t c", c=QUART)

        def flat(ap):
            return ap.rearrange("p q t c -> p (q t c)")

        for qs in pieces:
            js = cols_of(qs, QUART)
            for t in range(PACK):
                window = h_all[:, t * S : (t + 2) * S]
                nc.scalar.activation(out=far[:, t, js], in_=window.indirect(n5_l[:, cols_of(qs, QUART // 16)]), func=ACT.Copy)
            nc.vector.tensor_tensor(
                out=diff[:, qs], in0=by_quarter(far[:, :, js]), in1=by_quarter(h_view[:, :, js]), op=ALU.subtract
            )
            if qs.stop == 4:
                nc.scalar.activation(out=flat(dist[:, qs]), in_=flat(diff[:, qs]), func=ACT.Abs)
            else:
                nc.vector.scalar_tensor_tensor(
                    out=flat(dist[:, qs]), in0=flat(diff[:, qs]), scalar=-1.0, in1=flat(diff[:, qs]), op0=ALU.mult, op1=ALU.max
                )
        for qs in pieces:
            nc.scalar.activation(out=flat(logs[:, qs]), in_=flat(dist[:, qs]), func=ACT.Ln, bias=half_col[:])
        numer = sbt("numer", [P, PACK, S], F32, tag="far_then_numer")
        for u in range(2):
            js = slice(u * HALF, (u + 1) * HALF)
            ls = slice(u * HALF // 16, (u + 1) * HALF // 16)
            near = sbt(f"near{u}", [P, PACK, HALF], F32, tag="diff_then_near" if u else None)
            for t in range(PACK):
                nc.vector.tensor_copy(out=near[:, t, :], in_=h_all[:, t * S : (t + 2) * S].indirect(n4_l[:, ls]))
            nc.vector.tensor_tensor(out=numer[:, :, js], in0=h_view[:, :, js], in1=near[:], op=ALU.subtract)
        y_codes = sbt("y_codes", [P, S], U32)
        y_plane = sbt("y_plane", [P, S], U8)
        y_bf = sbt("y_bf", [P, S * PACK], BF16)
        out_view = out_0.rearrange("(p t) j -> p t j", t=PACK)
        recip = dist[:].rearrange("p t q c -> p t (q c)")
        for qs in [slice(q, q + 1) for q in range(4)]:
            js = cols_of(qs, QUART)
            nc.scalar.activation(out=by_quarter(recip[:, :, js]), in_=logs[:, qs], func=ACT.Exp, scale=-1.0)
            nc.vector.tensor_tensor(out=y[:, :, js], in0=numer[:, :, js], in1=recip[:, :, js], op=ALU.mult)
            bf = y_bf[:, cols_of(qs, QUART * PACK)]
            y_walk = y[:, :, js].rearrange("p t (c i) -> p c t i", i=4)
            if qs.start < 2:
                nc.scalar.copy(out=walk_dst(bf), in_=y_walk)
            else:
                nc.vector.tensor_copy(out=walk_dst(bf), in_=y_walk)
            nc.vector.quantize_mx(out=y_codes[:, js].bitcast(FP8X4), scales=y_plane[:, js], in_=bf)
            if qs.stop % 2 == 0:
                hs = slice(js.stop - HALF, js.stop)
                nc.sync.dma_start(out_view[:, :, hs], y[:, :, hs])
                nc.sync.dma_start(words_of(out_1)[:, hs], y_codes[:, hs].bitcast(I32))
        for q in range(4):
            eng = nc.scalar if q % 2 else nc.sync
            eng.dma_start(out_2[0, 4 * q : 4 * q + 4, :].bitcast(I32), y_plane[32 * q : 32 * q + 4, :].bitcast(I32))
